import numpy as np, ml_dtypes
CORES = [0,4,1,5,2,6,3,7]
N = 8
def setup_inputs(rng):
    return {"x": rng.standard_normal((N, 128, 4096), dtype=np.float32).astype(ml_dtypes.bfloat16)}
def reference(x):
    s = x.sum(axis=0, dtype=np.float64).astype(x.dtype)
    return {"y": np.broadcast_to(s, (N,) + s.shape)}

@@ -1,0 +1,58 @@
+from concourse.bass import DstId, RemoteDMATransfer
+
+P = 128
+COLS = 4096
+Q = COLS // 4
+
+SCRATCH = {
+    "xs": ("sbuf", [P, COLS], "bfloat16"),
+    "land": ("sbuf", [P, 3 * Q], "bfloat16"),
+    "peer": ("sbuf", [P, Q], "bfloat16"),
+    "out": ("sbuf", [P, COLS], "bfloat16"),
+}
+SEMAPHORES = ["local", "sent", "rs", "xd", "ag"]
+
+
+def rank_program(g, core, T, topo):
+    if T.rank_of(core) is None:
+        return
+    mine = sorted(c for c in T.cores if topo.die(c) == topo.die(core))
+    other = sorted(c for c in T.cores if topo.die(c) != topo.die(core))
+    q = mine.index(core)
+    partner = other[q]
+    mates = [c for c in mine if c != core]
+
+    def dst(c):
+        rid, pid, _se = topo.addr(c)
+        return DstId(rid=rid, pnc=pid)
+
+    def quarter(t, j):
+        return t[:, j * Q:(j + 1) * Q]
+
+    g.dma_start(T.xs[:], T.x[:]).then_inc(T.sem.local, 16)
+    g.wait_ge(T.sem.local, 16)
+
+    g.remote_dma_fused(
+        [RemoteDMATransfer(dst_ids=[dst(m)], dma_engine_mask=0xF << (4 * k), remote_sem=T.sem.rs,
+                           src=quarter(T.xs, mine.index(m)), dst=quarter(T.land, (q - mine.index(m) - 1) % 4))
+         for k, m in enumerate(mates)],
+        local_sem=T.sem.sent)
+    g.wait_ge(T.sem.rs, 3 * 4)
+
+    pieces = [quarter(T.xs, q)] + [quarter(T.land, s) for s in range(3)]
+    g.remote_dma_fused(
+        [RemoteDMATransfer(dst_ids=[dst(partner)], dma_engine_mask=0xFFFF, remote_sem=T.sem.xd,
+                           srcs=pieces, dsts=[T.peer[:]], alu_op=1)],
+        local_sem=T.sem.sent)
+    g.wait_ge(T.sem.xd, 16)
+
+    to = mates + [partner]
+    g.remote_dma_fused(
+        [RemoteDMATransfer(dst_ids=[dst(c) for c in to], dma_engine_mask=0xFFFF, remote_sem=T.sem.ag,
+                           srcs=pieces + [T.peer[:]], dsts=[quarter(T.out, q) for c in to], alu_op=1)],
+        local_sem=T.sem.sent)
+    g.wait_ge(T.sem.ag, 4 * 16)
+
+    g.dma_start(T.y[:], T.out[:]).then_inc(T.sem.local, 16)
+    g.wait_ge(T.sem.local, 32)
+    g.wait_ge(T.sem.sent, 12 + 16 + 16)

@@ -1,4 +1,5 @@
 from concourse.bass import DstId, RemoteDMATransfer
+from concourse.mybir import AluOpType
 
 P = 128
 COLS = 4096
@@ -6,11 +7,12 @@ Q = COLS // 4
 
 SCRATCH = {
     "xs": ("sbuf", [P, COLS], "bfloat16"),
+    "part": ("sbuf", [P, Q], "bfloat16"),
     "land": ("sbuf", [P, 3 * Q], "bfloat16"),
     "peer": ("sbuf", [P, Q], "bfloat16"),
     "out": ("sbuf", [P, COLS], "bfloat16"),
 }
-SEMAPHORES = ["local", "sent", "rs", "xd", "ag"]
+SEMAPHORES = ["ld", "ps", "ys", "st", "sent", "rs", "xd", "ag"]
 
 
 def rank_program(g, core, T, topo):
@@ -21,6 +23,8 @@ def rank_program(g, core, T, topo):
     q = mine.index(core)
     partner = other[q]
     mates = [c for c in mine if c != core]
+    sem = T.sem
+    add = AluOpType.add
 
     def dst(c):
         rid, pid, _se = topo.addr(c)
@@ -29,30 +33,45 @@ def rank_program(g, core, T, topo):
     def quarter(t, j):
         return t[:, j * Q:(j + 1) * Q]
 
-    g.dma_start(T.xs[:], T.x[:]).then_inc(T.sem.local, 16)
-    g.wait_ge(T.sem.local, 16)
+    g.dma_start(T.xs[:], T.x[:]).then_inc(sem.ld, 16)
+    g.dma_start(T.part[:], quarter(T.x, q)).then_inc(sem.ld, 16)
+    g.wait_ge(sem.ld, 32)
 
     g.remote_dma_fused(
-        [RemoteDMATransfer(dst_ids=[dst(m)], dma_engine_mask=0xF << (4 * k), remote_sem=T.sem.rs,
+        [RemoteDMATransfer(dst_ids=[dst(m)], dma_engine_mask=0xF << (4 * k), remote_sem=sem.rs,
                            src=quarter(T.xs, mine.index(m)), dst=quarter(T.land, (q - mine.index(m) - 1) % 4))
          for k, m in enumerate(mates)],
-        local_sem=T.sem.sent)
-    g.wait_ge(T.sem.rs, 3 * 4)
+        local_sem=sem.sent)
+    g.wait_ge(sem.rs, 3 * 4)
 
     pieces = [quarter(T.xs, q)] + [quarter(T.land, s) for s in range(3)]
     g.remote_dma_fused(
-        [RemoteDMATransfer(dst_ids=[dst(partner)], dma_engine_mask=0xFFFF, remote_sem=T.sem.xd,
+        [RemoteDMATransfer(dst_ids=[dst(partner)], dma_engine_mask=0xFFFF, remote_sem=sem.xd,
                            srcs=pieces, dsts=[T.peer[:]], alu_op=1)],
-        local_sem=T.sem.sent)
-    g.wait_ge(T.sem.xd, 16)
+        local_sem=sem.sent)
+    g.dma_start(quarter(T.y, q), quarter(T.land, 0)).then_inc(sem.ys, 16)
+    g.dma_start(T.part[:], quarter(T.land, 1), accum_op=add).then_inc(sem.ps, 16)
+    g.wait_ge(sem.xd, 16)
 
-    to = mates + [partner]
     g.remote_dma_fused(
-        [RemoteDMATransfer(dst_ids=[dst(c) for c in to], dma_engine_mask=0xFFFF, remote_sem=T.sem.ag,
-                           srcs=pieces + [T.peer[:]], dsts=[quarter(T.out, q) for c in to], alu_op=1)],
-        local_sem=T.sem.sent)
-    g.wait_ge(T.sem.ag, 4 * 16)
+        [RemoteDMATransfer(dst_ids=[dst(m) for m in mates], dma_engine_mask=0xFFFF, remote_sem=sem.ag,
+                           srcs=pieces + [T.peer[:]], dsts=[quarter(T.out, q) for m in mates], alu_op=1)],
+        local_sem=sem.sent)
+    g.wait_ge(sem.ys, 16)
+    g.dma_start(quarter(T.y, q), T.peer[:], accum_op=add).then_inc(sem.ys, 16)
+    g.wait_ge(sem.ps, 16)
+    g.dma_start(T.part[:], quarter(T.land, 2), accum_op=add).then_inc(sem.ps, 16)
 
-    g.dma_start(T.y[:], T.out[:]).then_inc(T.sem.local, 16)
-    g.wait_ge(T.sem.local, 32)
-    g.wait_ge(T.sem.sent, 12 + 16 + 16)
+    g.wait_ge(sem.ag, 3 * 16)
+    stores = 0
+    for lo, hi in ((0, q * Q), ((q + 1) * Q, COLS)):
+        if lo < hi:
+            g.dma_start(T.y[:, lo:hi], T.out[:, lo:hi]).then_inc(sem.st, 16)
+            stores += 1
+    g.wait_ge(sem.ys, 32)
+    g.wait_ge(sem.ps, 32)
+    g.dma_start(quarter(T.y, q), T.part[:], accum_op=add).then_inc(sem.ys, 16)
+
+    g.wait_ge(sem.ys, 48)
+    g.wait_ge(sem.st, 16 * stores)
+    g.wait_ge(sem.sent, 12 + 16 + 16)

from concourse.bass import DstId, RemoteDMATransfer
from concourse.mybir import AluOpType

P = 128
COLS = 4096
Q = COLS // 4

SCRATCH = {
    "xs": ("sbuf", [P, COLS], "bfloat16"),
    "part": ("sbuf", [P, Q], "bfloat16"),
    "land": ("sbuf", [P, 3 * Q], "bfloat16"),
    "peer": ("sbuf", [P, Q], "bfloat16"),
    "out": ("sbuf", [P, COLS], "bfloat16"),
}
SEMAPHORES = ["ld", "ps", "ys", "st", "sent", "rs", "xd", "ag"]


def rank_program(g, core, T, topo):
    if T.rank_of(core) is None:
        return
    mine = sorted(c for c in T.cores if topo.die(c) == topo.die(core))
    other = sorted(c for c in T.cores if topo.die(c) != topo.die(core))
    q = mine.index(core)
    partner = other[q]
    mates = [c for c in mine if c != core]
    sem = T.sem
    add = AluOpType.add

    def dst(c):
        rid, pid, _se = topo.addr(c)
        return DstId(rid=rid, pnc=pid)

    def quarter(t, j):
        return t[:, j * Q:(j + 1) * Q]

    g.dma_start(T.xs[:], T.x[:]).then_inc(sem.ld, 16)
    g.dma_start(T.part[:], quarter(T.x, q)).then_inc(sem.ld, 16)
    g.wait_ge(sem.ld, 32)

    g.remote_dma_fused(
        [RemoteDMATransfer(dst_ids=[dst(m)], dma_engine_mask=0xF << (4 * k), remote_sem=sem.rs,
                           src=quarter(T.xs, mine.index(m)), dst=quarter(T.land, (q - mine.index(m) - 1) % 4))
         for k, m in enumerate(mates)],
        local_sem=sem.sent)
    g.wait_ge(sem.rs, 3 * 4)

    pieces = [quarter(T.xs, q)] + [quarter(T.land, s) for s in range(3)]
    g.remote_dma_fused(
        [RemoteDMATransfer(dst_ids=[dst(partner)], dma_engine_mask=0xFFFF, remote_sem=sem.xd,
                           srcs=pieces, dsts=[T.peer[:]], alu_op=1)],
        local_sem=sem.sent)
    g.dma_start(quarter(T.y, q), quarter(T.land, 0)).then_inc(sem.ys, 16)
    g.dma_start(T.part[:], quarter(T.land, 1), accum_op=add).then_inc(sem.ps, 16)
    g.wait_ge(sem.xd, 16)

    g.remote_dma_fused(
        [RemoteDMATransfer(dst_ids=[dst(m) for m in mates], dma_engine_mask=0xFFFF, remote_sem=sem.ag,
                           srcs=pieces + [T.peer[:]], dsts=[quarter(T.out, q) for m in mates], alu_op=1)],
        local_sem=sem.sent)
    g.wait_ge(sem.ys, 16)
    g.dma_start(quarter(T.y, q), T.peer[:], accum_op=add).then_inc(sem.ys, 16)
    g.wait_ge(sem.ps, 16)
    g.dma_start(T.part[:], quarter(T.land, 2), accum_op=add).then_inc(sem.ps, 16)

    g.wait_ge(sem.ag, 3 * 16)
    stores = 0
    for lo, hi in ((0, q * Q), ((q + 1) * Q, COLS)):
        if lo < hi:
            g.dma_start(T.y[:, lo:hi], T.out[:, lo:hi]).then_inc(sem.st, 16)
            stores += 1
    g.wait_ge(sem.ys, 32)
    g.wait_ge(sem.ps, 32)
    g.dma_start(quarter(T.y, q), T.part[:], accum_op=add).then_inc(sem.ys, 16)

    g.wait_ge(sem.ys, 48)
    g.wait_ge(sem.st, 16 * stores)
    g.wait_ge(sem.sent, 12 + 16 + 16)
